import numpy as np
import ml_dtypes


def mxq(x, axis, fmt="e4m3"):
    dtype, down = {"e4m3": (ml_dtypes.float8_e4m3fn, 7), "e5m2": (ml_dtypes.float8_e5m2, 14)}[fmt]
    v = np.moveaxis(np.asarray(x, np.float32).astype(ml_dtypes.bfloat16).astype(np.float64), axis, -1)
    blocks = v.reshape(v.shape[:-1] + (-1, 32))
    amax = np.abs(blocks).max(-1, keepdims=True)
    byte = np.maximum(np.where(amax > 0, np.frexp(amax)[1] - 1 + 127, 0) - down, 1)
    scale = np.exp2(byte - 127.0)
    codes = (blocks / scale).astype(np.float32).astype(dtype).astype(np.float64)
    return np.moveaxis((codes * scale).reshape(v.shape), -1, axis)


WIDE = False


def mx_kscale(k):
    if not WIDE:
        return np.ones(k)
    levels = np.array([10, -10, 5, -5, 0])
    if k % 512:
        return np.exp2(np.random.permutation(np.resize(levels, k // 32))).repeat(32)
    a = np.empty((k // 512, 16))
    for p in range(k // 512):
        a[p, :8] = np.random.permutation(np.resize(levels, 8))
        for g in range(8):
            far = levels[np.abs(levels - a[p, g]) >= 10]
            a[p, g + 8] = far[np.random.randint(len(far))]
    return np.exp2(a.ravel()).repeat(32)


BF16 = ml_dtypes.bfloat16


def bf(x):
    return np.asarray(x, np.float32).astype(BF16)


def f64(x):
    return np.asarray(x).astype(np.float64)


E2M1 = np.array([0.0, 0.5, 1.0, 1.5, 2.0, 3.0, 4.0, 6.0, -0.0, -0.5, -1.0, -1.5, -2.0, -3.0, -4.0, -6.0])


def pack_weight(w, fmt):
    k, n = w.shape
    w = f64(bf(w)).reshape(k // 32, 32, n)
    amax = np.abs(w).max(1)
    if fmt == "e4m3":
        byte = np.frexp(amax)[1] - 1 + 127 - 7
    else:
        mant, ex = np.frexp(amax / 6.0)
        byte = np.where(mant > 0.5, ex, ex - 1) + 127
    byte = np.clip(np.where(amax > 0, byte, 1), 1, 254)
    scaled = (w * np.exp2(127.0 - byte)[:, None, :]).reshape(k, n).astype(np.float32)
    by_word = np.ascontiguousarray(scaled.reshape(k // 512, 128, 4, n).transpose(0, 1, 3, 2))
    if fmt == "e4m3":
        words = by_word.astype(ml_dtypes.float8_e4m3fn).view(np.uint8)
    else:
        c = by_word.astype(ml_dtypes.float4_e2m1fn).view(np.uint8) & 0xF
        words = c[..., 0::2] | (c[..., 1::2] << 4)
    return np.ascontiguousarray(words), np.ascontiguousarray(byte.astype(np.uint8).reshape(k // 512, 16, n))


def unpack_weight(words, scales, fmt):
    g, p, n, _ = words.shape
    if fmt == "e4m3":
        vals = np.ascontiguousarray(words).view(ml_dtypes.float8_e4m3fn).astype(np.float64)
    else:
        nib = np.empty((g, p, n, 4), np.uint8)
        nib[..., 0::2] = words & 0xF
        nib[..., 1::2] = words >> 4
        vals = E2M1[nib]
    vals = vals * np.repeat(np.exp2(scales.astype(np.float64) - 127.0), 8, axis=1)[..., None]
    return vals.transpose(0, 1, 3, 2).reshape(g * 512, n)
def pack4(w):
    words, scales = pack_weight(w, "e2m1")
    return words.reshape(words.shape[0], 128, -1), scales


def unpack4(words, scales):
    return unpack_weight(words.reshape(words.shape[0], 128, -1, 2), scales, "e2m1")


M, D, F = 1024, 1024, 1536

SD = 0.5


def silu(z):
    return 0.5 * z * (1.0 + np.tanh(0.5 * z))


def setup_inputs():
    s, t = mx_kscale(D), mx_kscale(F)
    sigma = np.exp(0.8 * np.random.standard_normal(M))
    lo = sigma * np.random.uniform(0.1, 0.6, M)
    x = np.random.standard_normal((M, D)) * np.sqrt(sigma ** 2 + SD ** 2)[:, None]
    w_gate = np.random.standard_normal((D, F)) / np.sqrt(D) / s[:, None]
    w_value = np.random.standard_normal((D, F)) / np.sqrt(D) / s[:, None] * t
    w1_words, w1_scales = pack4(np.concatenate([w_gate, w_value], axis=1))
    w2 = 1.5 * np.random.standard_normal((F, D)) / np.sqrt(F) / t[:, None]
    w2_words, w2_scales = pack_weight(w2, "e4m3")
    return {"x": bf(x),
            "sigma": bf(sigma),
            "sigma_lo": bf(lo),
            "in_gain": bf((1.0 + 0.1 * np.random.standard_normal(D)) * s),
            "w1_words": w1_words,
            "w1_scales": w1_scales,
            "e_mul": bf(np.random.standard_normal(F)),
            "e_add": bf(np.random.standard_normal(F)),
            "b_gate": bf(0.3 * np.random.standard_normal(F)),
            "b_value": bf(0.3 * np.random.standard_normal(F) * t),
            "w2_words": w2_words,
            "w2_scales": w2_scales,
            "b_out": bf(0.3 * np.random.standard_normal(D))}


def reference(x, sigma, sigma_lo, in_gain, w1_words, w1_scales, e_mul, e_add, b_gate, b_value, w2_words, w2_scales, b_out):
    xx = f64(x)
    sig = f64(sigma)[:, None]
    gap = sig - f64(sigma_lo)[:, None]
    c_in = 1.0 / np.sqrt(sig ** 2 + SD ** 2)
    c_noise = 0.25 * np.log(sig)
    c_skip = SD ** 2 / (gap ** 2 + SD ** 2)
    c_out = SD * gap / np.sqrt(sig ** 2 + SD ** 2)
    u = xx * c_in * f64(in_gain)
    y = mxq(u, 1, "e4m3") @ unpack4(w1_words, w1_scales)
    gate = y[:, :F] * (1.0 + c_noise * f64(e_mul)) + c_noise * f64(e_add) + f64(b_gate)
    value = y[:, F:] + f64(b_value)
    h = silu(gate) * value
    net = (mxq(h, 1, "e4m3") @ unpack_weight(w2_words, w2_scales, "e4m3")) + f64(b_out)
    return c_skip * xx + c_out * net

@@ -1,0 +1,460 @@
+from contextlib import ExitStack
+
+import concourse.mybir as mybir
+from concourse.masks import make_identity
+
+F32 = mybir.dt.float32
+BF16 = mybir.dt.bfloat16
+U32 = mybir.dt.uint32
+I32 = mybir.dt.int32
+U8 = mybir.dt.uint8
+FP8X4 = mybir.dt.float8_e4m3fn_x4
+FP4X4 = mybir.dt.float4_e2m1fn_x4
+ALU = mybir.AluOpType
+ACT = mybir.ActivationFunctionType
+
+M, D, F = 1024, 1024, 1536
+P = 128
+HALF = 512
+NF = F // P
+
+UNITS = 2 * NF
+FLOPS = 2 * M * D * 2 * F + 2 * M * F * D
+
+
+def tile_multistep_consistency_head_f7_kernel(
+    tc, x, sigma, sigma_lo, in_gain, w1_words, w1_scales, e_mul, e_add, b_gate, b_value, w2_words, w2_scales, b_out, out
+):
+    nc = tc.nc
+    with ExitStack() as ctx:
+        keep = ctx.enter_context(tc.tile_pool(name="keep", bufs=1))
+        work = ctx.enter_context(tc.tile_pool(name="work", bufs=3))
+        ps = ctx.enter_context(tc.psum_pool(name="ps", bufs=1))
+        ctx.enter_context(tc.manual_schedule())
+
+        def bank(tag):
+            return ps.tile([P, HALF], F32, tag=tag, bufs={"g": 4, "v": 2, "o": 2}[tag], name="bank_" + tag)
+
+        vecs = keep.tile([P, P], BF16, align_bytes=64, name="vecs")
+        sv = keep.tile([P, P], BF16, align_bytes=64, name="sv")
+        gb = keep.tile([P, D], BF16, align_bytes=64, name="gb")
+        brows = keep.tile([P, D], BF16, align_bytes=64, name="brows")
+        ones = keep.tile([P, P], BF16, align_bytes=64, name="ones")
+        ident = keep.tile([P, P], F32, align_bytes=64, name="ident")
+        ident_b = keep.tile([P, P], BF16, align_bytes=64, name="ident_b")
+        x_t = keep.tile([P, 8, D], BF16, align_bytes=64, name="x_t")
+        u_t = keep.tile([P, 8, D], BF16, align_bytes=64, name="u_t")
+        pre = keep.tile([P, 8, D], F32, align_bytes=64, name="pre")
+        w1 = keep.tile([P, 2, 4 * F], U8, align_bytes=64, name="w1")
+        w1s = keep.tile([P, 2, 2 * F], U8, align_bytes=64, name="w1s")
+        w2 = keep.tile([P, 3, D], I32, align_bytes=64, name="w2")
+        w2s = keep.tile([P, 3, D], U8, align_bytes=64, name="w2s")
+        u_codes = keep.tile([P, 2, M], U32, align_bytes=64, name="u_codes")
+        u_scales = keep.tile([P, 2, M], U8, align_bytes=64, name="u_scales")
+        h_codes = keep.tile([P, 2, 3, HALF], U32, align_bytes=64, name="h_codes")
+        h_scales = keep.tile([P, 2, 3, HALF], U8, align_bytes=64, name="h_scales")
+        sl = keep.tile([P, 16], F32, align_bytes=64, name="sl")
+        cols = keep.tile([P, 48], F32, align_bytes=64, name="cols")
+        sig_b = keep.tile([P, 8], BF16, align_bytes=64, name="sig_b")
+        cn = keep.tile([P, M], F32, align_bytes=64, name="cn")
+        gain_bc = keep.tile([P, D], BF16, align_bytes=64, name="gain_bc")
+        parts = keep.tile([P, 8, P], BF16, align_bytes=64, name="parts")
+        rest = keep.tile([P, 8], F32, name="rest")
+        c_rows = keep.tile([P, 8 * P], BF16, align_bytes=64, name="c_rows")
+        dummy = keep.tile([P, 2], F32, align_bytes=64, name="dummy")
+        gap = keep.tile([P, 8], F32, name="gap")
+        s2 = keep.tile([P, 8], F32, name="s2")
+        g2 = keep.tile([P, 8], F32, name="g2")
+        rg = keep.tile([P, 8], F32, name="rg")
+        c_in = keep.tile([P, 8], F32, name="c_in")
+        c_skip = keep.tile([P, 8], F32, name="c_skip")
+        c_out = keep.tile([P, 8], F32, name="c_out")
+        mhalf = keep.tile([P, 8], F32, name="mhalf")
+
+        nc.vector.memset(sv[:], 0.0)
+        nc.vector.memset(gb[:], 0.0)
+        nc.vector.memset(dummy[:], 1.0)
+        nc.vector.memset(ones[:], 1.0)
+        nc.vector.memset(w1s[:].bitcast(I32), 0)
+        make_identity(nc, ident[:])
+        nc.gpsimd.memset(mhalf[:], -0.5)
+        nc.gpsimd.memset(vecs[:].bitcast(I32), 0)
+        nc.gpsimd.memset(brows[:].bitcast(I32), 0)
+        nc.gpsimd.memset(w2s[:].bitcast(I32), 0)
+        nc.gpsimd.memset(parts[:].bitcast(I32), 0)
+        nc.scalar.activation(out=dummy[:, 1:2], in_=dummy[:, 0:1], func=ACT.Ln)
+
+        def load_vec(t, v, row, n):
+            nc.sync.dma_start(out=t[row : row + n, :], in_=v.rearrange("(j p) -> j p", p=P))
+
+        def load_x(r0, n):
+            nc.sync.dma_start(
+                out=x_t[:, r0 : r0 + n, :], in_=x[r0 * P : (r0 + n) * P, :].rearrange("(n p) d -> p n d", p=P)
+            )
+
+        def load_w1(c0, n):
+            nc.sync.dma_start(
+                out=w1[:, :, 2 * c0 : 2 * (c0 + n)].bitcast(I32),
+                in_=w1_words[:, :, 2 * c0 : 2 * (c0 + n)].rearrange("g p b -> p g b").bitcast(I32),
+            )
+
+        def load_scales(plane, scales):
+            for q in range(4):
+                nc.sync.dma_start(
+                    out=plane[32 * q : 32 * q + 4, :, :].bitcast(I32),
+                    in_=scales[:, 4 * q : 4 * q + 4, :].rearrange("g q n -> q g n").bitcast(I32),
+                )
+
+        load_vec(sv, sigma, 0, 8)
+        load_vec(sv, sigma_lo, 8, 8)
+        nc.sync.dma_start(out=gb[0:1, :], in_=in_gain.unsqueeze(0))
+        load_x(0, 1)
+        load_x(1, 1)
+        load_x(2, 2)
+        load_vec(vecs, e_mul, 0, 12)
+        load_vec(vecs, e_add, 12, 12)
+        load_vec(vecs, b_gate, 24, 12)
+        load_vec(vecs, b_value, 36, 12)
+        load_scales(w1s, w1_scales)
+        load_w1(0, 512)
+        load_w1(F, 512)
+        load_x(4, 2)
+        load_x(6, 2)
+        nc.sync.dma_start(out=brows[0:3, :], in_=b_out.partition_broadcast(3))
+        for g in (1, 2):
+            load_w1(512 * g, 512)
+            load_w1(F + 512 * g, 512)
+        load_scales(w2s, w2_scales)
+        for g in range(3):
+            nc.sync.dma_start(out=w2[:, g, :], in_=w2_words[g].rearrange("p n t -> p (n t)").bitcast(I32))
+
+        nc.vector.tensor_copy(out=ident_b[:], in_=ident[:])
+        vb = bank("o")
+        nc.tensor.transpose(vb[:].bitcast(BF16)[:, 0:P], sv[:], ident_b[:])
+        nc.vector.tensor_copy(out=sl[:], in_=vb[:].bitcast(BF16)[:, 0:16])
+        sig = sl[:, 0:8]
+        nc.vector.tensor_tensor(out=s2[:], in0=sig, in1=sig, op=ALU.mult)
+        nc.vector.tensor_copy(out=sig_b[:], in_=vb[:].bitcast(BF16)[:, 0:8])
+        nc.vector.tensor_scalar(out=s2[:], in0=s2[:], scalar1=0.25, scalar2=None, op0=ALU.add)
+        nc.gpsimd.tensor_tensor(out=c_in[:], in0=s2[:], in1=mhalf[:], op=ALU.pow)
+        gbank = [bank("v"), bank("v")]
+        for c in range(2):
+            nc.tensor.matmul(gbank[c][:], ones[:], gb[:, c * HALF : (c + 1) * HALF], start=True, stop=True)
+        sbank = [bank("g"), bank("g")]
+        for rt in range(8):
+            nc.tensor.matmul(
+                sbank[rt // 4][:, (rt % 4) * P : (rt % 4 + 1) * P],
+                sig_b[:, rt : rt + 1].to_broadcast([P, P]),
+                ident_b[:],
+                start=True,
+                stop=True,
+            )
+        for c in range(2):
+            nc.scalar.activation(out=cn[:, c * HALF : (c + 1) * HALF], in_=sbank[c][:], func=ACT.Ln)
+
+        def feature_columns():
+            fb = bank("o")
+            nc.tensor.transpose(fb[:].bitcast(BF16)[:, 0:P], vecs[:], ident_b[:])
+            nc.vector.tensor_scalar(
+                out=cols[:, 0:24], in0=fb[:].bitcast(BF16)[:, 0:24], scalar1=0.25, scalar2=None, op0=ALU.mult
+            )
+            nc.vector.tensor_copy(out=cols[:, 24:48], in_=fb[:].bitcast(BF16)[:, 24:48])
+
+        def keep_gain(c):
+            nc.scalar.copy(out=gain_bc[:, c * HALF : (c + 1) * HALF], in_=gbank[c][:])
+
+        def late_coefficients():
+            nc.vector.tensor_tensor(out=gap[:], in0=sig, in1=sl[:, 8:16], op=ALU.subtract)
+            nc.vector.tensor_tensor(out=g2[:], in0=gap[:], in1=gap[:], op=ALU.mult)
+            nc.vector.scalar_tensor_tensor(
+                out=c_out[:], in0=gap[:], scalar=0.5, in1=c_in[:], op0=ALU.mult, op1=ALU.mult
+            )
+            nc.vector.tensor_scalar(out=g2[:], in0=g2[:], scalar1=0.25, scalar2=None, op0=ALU.add)
+            nc.vector.tensor_copy(out=parts[:, :, 0], in_=c_out[:])
+            nc.vector.reciprocal(out=rg[:], in_=g2[:])
+            nc.vector.tensor_tensor(out=rest[:], in0=c_out[:], in1=parts[:, :, 0], op=ALU.subtract)
+            nc.vector.tensor_scalar(out=c_skip[:], in0=rg[:], scalar1=0.25, scalar2=None, op0=ALU.mult)
+            nc.vector.tensor_copy(out=parts[:, :, 1], in_=rest[:])
+            nc.vector.tensor_tensor(out=parts[:, :, 2], in0=rest[:], in1=parts[:, :, 1], op=ALU.subtract)
+
+        def make_u(rt, c, src):
+            nc.vector.scalar_tensor_tensor(
+                out=u_t[:, rt, c * HALF : (c + 1) * HALF],
+                in0=x_t[:, rt, c * HALF : (c + 1) * HALF],
+                scalar=c_in[:, rt : rt + 1],
+                in1=src,
+                op0=ALU.mult,
+                op1=ALU.mult,
+            )
+
+        xc = {}
+
+        def scale_x(rt):
+            xc[rt] = work.tile([P, D], F32, align_bytes=64, name="xc", bufs=2)
+            nc.scalar.activation(out=xc[rt][:], in_=x_t[:, rt, :], func=ACT.Copy, scale=c_in[:, rt : rt + 1])
+
+        def gain_x(rt, c):
+            cs = slice(c * HALF, (c + 1) * HALF)
+            nc.gpsimd.tensor_tensor(out=u_t[:, rt, cs], in0=xc[rt][:, cs], in1=gain_bc[:, cs], op=ALU.mult)
+
+        ug = {}
+
+        def turn_u(rt, tag="o"):
+            xb = bank(tag)
+            words = u_t[:, rt, :].bitcast(F32)
+            for g in range(2):
+                for u in range(2):
+                    i = 2 * g + u
+                    nc.tensor.transpose(xb[:, i * P : (i + 1) * P], words[:, 256 * g + u : 256 * (g + 1) : 2], ident[:])
+            ug[rt] = xb
+
+        def copy_u(rt):
+            grouped = work.tile([P, 2, P, 4], BF16, align_bytes=64, name="ug")
+            nc.scalar.copy(
+                out=grouped[:].bitcast(F32),
+                in_=ug[rt][:].rearrange("p (g u r) -> p g r u", g=2, u=2),
+            )
+            ug[rt] = grouped
+
+        def quant_u(rt):
+            for g in range(2):
+                nc.vector.quantize_mx(
+                    out=u_codes[:, g, rt * P : (rt + 1) * P].bitcast(FP8X4),
+                    scales=u_scales[:, g, rt * P : (rt + 1) * P],
+                    in_=ug[rt][:, g].rearrange("p r t -> p (r t)"),
+                )
+
+        def turn_c():
+            cb = bank("o")
+            for rt in range(8):
+                nc.tensor.transpose(cb[:].bitcast(BF16)[:, rt * P : (rt + 1) * P], parts[:, rt, :], ident_b[:])
+            nc.scalar.copy(out=c_rows[:], in_=cb[:].bitcast(BF16))
+
+        pb = {}
+
+        def bias_mm(rt, c):
+            pb[rt, c] = bank("o")
+            nc.tensor.matmul(
+                pb[rt, c][:], c_rows[:, rt * P : (rt + 1) * P], brows[:, c * HALF : (c + 1) * HALF], start=True, stop=True
+            )
+
+        def make_pre(rt, c):
+            cs = slice(c * HALF, (c + 1) * HALF)
+            nc.vector.scalar_tensor_tensor(
+                out=pre[:, rt, cs],
+                in0=x_t[:, rt, cs],
+                scalar=c_skip[:, rt : rt + 1],
+                in1=pb[rt, c][:],
+                op0=ALU.mult,
+                op1=ALU.add,
+            )
+
+        def stage1(k, col0, tag):
+            hb, j = divmod(k, NF)
+            b = bank(tag)
+            c0 = col0 + P * j
+            for g in range(2):
+                nc.tensor.matmul_mx(
+                    out=b[:],
+                    lhsT=w1[:, g, 2 * c0 : 2 * (c0 + P)].bitcast(FP4X4),
+                    lhsT_scale=w1s[:, g, c0 : c0 + P],
+                    rhs=u_codes[:, g, hb * HALF : (hb + 1) * HALF].bitcast(FP8X4),
+                    rhs_scale=u_scales[:, g, hb * HALF : (hb + 1) * HALF],
+                    start=(g == 0),
+                    stop=(g == 1),
+                )
+            return b
+
+        gate, value, t_of, z_of, s_of = {}, {}, {}, {}, {}
+        hd, hg = {}, {}
+
+        def op_gate(k):
+            gate[k] = stage1(k, 0, "g")
+
+        def op_value(k):
+            value[k] = stage1(k, F, "v")
+
+        def op_t(k):
+            j = k % NF
+            t = work.tile([P, HALF], F32, align_bytes=64, name="t", bufs=4)
+            nc.scalar.activation(
+                out=t[:], in_=gate[k][:], func=ACT.Identity, scale=cols[:, j : j + 1], bias=cols[:, 12 + j : 13 + j]
+            )
+            t_of[k] = t
+
+        def op_t2(k):
+            hb = k // NF
+            t2 = work.tile([P, HALF], F32, align_bytes=64, name="t2", bufs=4)
+            nc.gpsimd.tensor_tensor(out=t2[:], in0=t_of[k][:], in1=cn[:, hb * HALF : (hb + 1) * HALF], op=ALU.mult)
+            t_of[k] = t2
+
+        def op_z(k):
+            z = work.tile([P, HALF], F32, align_bytes=64, name="z", bufs=4)
+            nc.vector.tensor_tensor(out=z[:], in0=gate[k][:], in1=t_of[k][:], op=ALU.add)
+            z_of[k] = z
+
+        def op_s(k):
+            j = k % NF
+            s = work.tile([P, HALF], F32, align_bytes=64, name="s", bufs=4)
+            nc.scalar.activation(out=s[:], in_=z_of[k][:], func=ACT.Silu, bias=cols[:, 24 + j : 25 + j])
+            s_of[k] = s
+
+        def op_h(k):
+            j = k % NF
+            h = work.tile([P, HALF], BF16, align_bytes=64, name="h", bufs=6)
+            nc.vector.scalar_tensor_tensor(
+                out=h[:],
+                in0=value[k][:],
+                scalar=cols[:, 36 + j : 37 + j],
+                in1=s_of[k][:],
+                op0=ALU.add,
+                op1=ALU.mult,
+            )
+            q, jj = divmod(k, 4)
+            if jj == 0:
+                hd[q] = work.tile([P, 4, HALF], BF16, align_bytes=64, name="hd")
+            for t in range(4):
+                nc.sync.dma_start(out=hd[q][32 * jj : 32 * jj + 32, t, :], in_=h[t:P:4, :])
+
+        def weave(q, eng, r0, r1):
+            if q not in hg:
+                hg[q] = work.tile([P, HALF, 4], BF16, align_bytes=64, name="hg")
+            dst = hg[q][:, r0:r1, :]
+            src = hd[q][:, :, r0:r1].rearrange("p t r -> p r t")
+            if eng == "g":
+                nc.gpsimd.tensor_scalar(out=dst, in0=src, scalar1=1.0, scalar2=0.0, op0=ALU.mult, op1=ALU.add)
+            elif eng == "a":
+                nc.scalar.copy(out=dst, in_=src)
+            else:
+                nc.vector.tensor_copy(out=dst, in_=src)
+
+        def quant_h(q, r0, r1):
+            hb, g = divmod(q, 3)
+            nc.vector.quantize_mx(
+                out=h_codes[:, hb, g, r0:r1].bitcast(FP8X4),
+                scales=h_scales[:, hb, g, r0:r1],
+                in_=hg[q][:, r0:r1, :].rearrange("p r t -> p (r t)"),
+            )
+
+        obank = {}
+
+        def stage2(hb, i, gs, tag=None):
+            r, c = divmod(i, 2)
+            if tag is not None:
+                obank[hb, i] = bank(tag)
+            for g in gs:
+                nc.tensor.matmul_mx(
+                    out=obank[hb, i][:],
+                    lhsT=h_codes[:, hb, g, r * P : (r + 1) * P].bitcast(FP8X4),
+                    lhsT_scale=h_scales[:, hb, g, r * P : (r + 1) * P],
+                    rhs=w2[:, g, c * HALF : (c + 1) * HALF].bitcast(FP8X4),
+                    rhs_scale=w2s[:, g, c * HALF : (c + 1) * HALF],
+                    start=(g == 0),
+                    stop=(g == 2),
+                )
+
+        def store(rt, c, o):
+            nc.sync.dma_start(out=out[rt * P : (rt + 1) * P, c * HALF : (c + 1) * HALF], in_=o[:])
+
+        def finish(hb, i):
+            r, c = divmod(i, 2)
+            rt = 4 * hb + r
+            o = work.tile([P, HALF], F32, align_bytes=64, name="o", bufs=8)
+            nc.vector.scalar_tensor_tensor(
+                out=o[:],
+                in0=obank[hb, i][:],
+                scalar=c_out[:, rt : rt + 1],
+                in1=pre[:, rt, c * HALF : (c + 1) * HALF],
+                op0=ALU.mult,
+                op1=ALU.add,
+            )
+            store(rt, c, o)
+
+        def finish_ag(hb, i):
+            r, c = divmod(i, 2)
+            rt = 4 * hb + r
+            o1 = work.tile([P, HALF], F32, align_bytes=64, name="o1")
+            o = work.tile([P, HALF], F32, align_bytes=64, name="o", bufs=8)
+            nc.scalar.activation(out=o1[:], in_=obank[hb, i][:], func=ACT.Copy, scale=c_out[:, rt : rt + 1])
+            nc.gpsimd.tensor_tensor(out=o[:], in0=o1[:], in1=pre[:, rt, c * HALF : (c + 1) * HALF], op=ALU.add)
+            store(rt, c, o)
+
+        for rt in range(4):
+            for c in range(2):
+                make_u(rt, c, gbank[c][:])
+            turn_u(rt, "og"[rt % 2])
+            copy_u(rt)
+            if rt < 2:
+                keep_gain(rt)
+        nc.scalar.activation(out=dummy[:, 1:2], in_=dummy[:, 0:1], func=ACT.Silu)
+        for rt in range(4):
+            quant_u(rt)
+        feature_columns()
+
+        table = {}
+
+        def at(k, fn, *args):
+            table.setdefault(k, []).append((fn, args))
+
+        for n, rt in enumerate((4, 5)):
+            at(2 * n, make_u, rt, 0, gain_bc[:, 0:HALF])
+            at(2 * n + 1, make_u, rt, 1, gain_bc[:, HALF:D])
+            at(2 * n + 2, turn_u, rt)
+            at(2 * n + 3, copy_u, rt)
+            at(2 * n + 4, quant_u, rt)
+        for n, rt in enumerate((6, 7)):
+            at(3 * n, scale_x, rt)
+            at(3 * n + 1, gain_x, rt, 0)
+            at(3 * n + 3, gain_x, rt, 1)
+            at(3 * n + 4, turn_u, rt)
+            at(3 * n + 5, copy_u, rt)
+            at(3 * n + 6, quant_u, rt)
+        at(0, turn_c)
+        for n in range(16):
+            rt, c = divmod(n, 2)
+            at(n + 1, bias_mm, rt, c)
+            at(n + 2, make_pre, rt, c)
+        for q in range(5):
+            s = 4 * q + 8
+            at(s, weave, q, "g", 0, 128)
+            at(s, weave, q, "a", 128, 256)
+            at(s + 1, weave, q, "g", 256, 384)
+            at(s + 1, weave, q, "a", 384, 512)
+            at(s + 2, quant_h, q, 0, HALF)
+        for i in range(8):
+            at(18 + i, stage2, 0, i, (0, 1, 2), "o")
+            at(19 + i, finish, 0, i)
+
+        def unit(fn, k):
+            if 0 <= k < UNITS:
+                fn(k)
+
+        for k in range(-2, UNITS + 3):
+            unit(op_gate, k + 2)
+            unit(op_s, k - 2)
+            unit(op_z, k - 1)
+            unit(op_h, k - 3)
+            unit(op_t, k + 1)
+            unit(op_t2, k)
+            unit(op_value, k - 1)
+            if k == -1:
+                late_coefficients()
+            for fn, args in table.get(k, []):
+                fn(*args)
+
+        tags = ["o", "o", "g", "g", "g", "g", "v", "v"]
+        for i in range(8):
+            stage2(1, i, (0, 1), tags[i])
+        weave(5, "v", 0, 128)
+        weave(5, "a", 128, 256)
+        weave(5, "g", 256, 384)
+        quant_h(5, 0, 128)
+        weave(5, "v", 384, 512)
+        for r in range(1, 4):
+            quant_h(5, 128 * r, 128 * (r + 1))
+        for i in range(8):
+            stage2(1, i, (2,))
+            if i % 3 == 1:
+                finish_ag(1, i)
+            else:
+                finish(1, i)

@@ -33,12 +33,12 @@ def tile_multistep_consistency_head_f7_kernel(
         ctx.enter_context(tc.manual_schedule())
 
         def bank(tag):
-            return ps.tile([P, HALF], F32, tag=tag, bufs={"g": 4, "v": 2, "o": 2}[tag], name="bank_" + tag)
+            return ps.tile([P, HALF], F32, tag=tag, bufs={"g": 3, "v": 2, "o": 2, "x": 1}[tag], name="bank_" + tag)
 
-        vecs = keep.tile([P, P], BF16, align_bytes=64, name="vecs")
+        vecs = keep.tile([P, 3 * P], BF16, align_bytes=64, name="vecs")
         sv = keep.tile([P, P], BF16, align_bytes=64, name="sv")
         gb = keep.tile([P, D], BF16, align_bytes=64, name="gb")
-        brows = keep.tile([P, D], BF16, align_bytes=64, name="brows")
+        brows = keep.tile([P, 2, D], BF16, align_bytes=64, name="brows")
         ones = keep.tile([P, P], BF16, align_bytes=64, name="ones")
         ident = keep.tile([P, P], F32, align_bytes=64, name="ident")
         ident_b = keep.tile([P, P], BF16, align_bytes=64, name="ident_b")
@@ -54,12 +54,12 @@ def tile_multistep_consistency_head_f7_kernel(
         h_codes = keep.tile([P, 2, 3, HALF], U32, align_bytes=64, name="h_codes")
         h_scales = keep.tile([P, 2, 3, HALF], U8, align_bytes=64, name="h_scales")
         sl = keep.tile([P, 16], F32, align_bytes=64, name="sl")
-        cols = keep.tile([P, 48], F32, align_bytes=64, name="cols")
+        cols = keep.tile([P, 4, NF], F32, align_bytes=64, name="cols")
         sig_b = keep.tile([P, 8], BF16, align_bytes=64, name="sig_b")
         cn = keep.tile([P, M], F32, align_bytes=64, name="cn")
-        gain_bc = keep.tile([P, D], BF16, align_bytes=64, name="gain_bc")
         parts = keep.tile([P, 8, P], BF16, align_bytes=64, name="parts")
         rest = keep.tile([P, 8], F32, name="rest")
+        ratio = keep.tile([P, 8], F32, name="ratio")
         c_rows = keep.tile([P, 8 * P], BF16, align_bytes=64, name="c_rows")
         dummy = keep.tile([P, 2], F32, align_bytes=64, name="dummy")
         gap = keep.tile([P, 8], F32, name="gap")
@@ -70,18 +70,21 @@ def tile_multistep_consistency_head_f7_kernel(
         c_skip = keep.tile([P, 8], F32, name="c_skip")
         c_out = keep.tile([P, 8], F32, name="c_out")
         mhalf = keep.tile([P, 8], F32, name="mhalf")
+        mone = keep.tile([P, 8], F32, name="mone")
 
+        make_identity(nc, ident[:])
         nc.vector.memset(sv[:], 0.0)
         nc.vector.memset(gb[:], 0.0)
         nc.vector.memset(dummy[:], 1.0)
         nc.vector.memset(ones[:], 1.0)
+        nc.vector.memset(vecs[:], 0.0)
         nc.vector.memset(w1s[:].bitcast(I32), 0)
-        make_identity(nc, ident[:])
+        nc.vector.memset(parts[:].bitcast(I32), 0)
+        nc.vector.memset(brows[:].bitcast(I32), 0)
+        nc.vector.memset(w2s[:].bitcast(I32), 0)
         nc.gpsimd.memset(mhalf[:], -0.5)
-        nc.gpsimd.memset(vecs[:].bitcast(I32), 0)
-        nc.gpsimd.memset(brows[:].bitcast(I32), 0)
-        nc.gpsimd.memset(w2s[:].bitcast(I32), 0)
-        nc.gpsimd.memset(parts[:].bitcast(I32), 0)
+        nc.gpsimd.memset(mone[:], -1.0)
+        nc.scalar.copy(out=ident_b[:], in_=ident[:])
         nc.scalar.activation(out=dummy[:, 1:2], in_=dummy[:, 0:1], func=ACT.Ln)
 
         def load_vec(t, v, row, n):
@@ -111,24 +114,13 @@ def tile_multistep_consistency_head_f7_kernel(
         load_x(0, 1)
         load_x(1, 1)
         load_x(2, 2)
-        load_vec(vecs, e_mul, 0, 12)
-        load_vec(vecs, e_add, 12, 12)
-        load_vec(vecs, b_gate, 24, 12)
-        load_vec(vecs, b_value, 36, 12)
         load_scales(w1s, w1_scales)
+        for v, vec in enumerate((e_mul, e_add, b_gate, b_value)):
+            nc.sync.dma_start(out=vecs[4 * v : 4 * v + 4, :], in_=vec.rearrange("(j p) -> j p", j=4))
         load_w1(0, 512)
         load_w1(F, 512)
         load_x(4, 2)
         load_x(6, 2)
-        nc.sync.dma_start(out=brows[0:3, :], in_=b_out.partition_broadcast(3))
-        for g in (1, 2):
-            load_w1(512 * g, 512)
-            load_w1(F + 512 * g, 512)
-        load_scales(w2s, w2_scales)
-        for g in range(3):
-            nc.sync.dma_start(out=w2[:, g, :], in_=w2_words[g].rearrange("p n t -> p (n t)").bitcast(I32))
-
-        nc.vector.tensor_copy(out=ident_b[:], in_=ident[:])
         vb = bank("o")
         nc.tensor.transpose(vb[:].bitcast(BF16)[:, 0:P], sv[:], ident_b[:])
         nc.vector.tensor_copy(out=sl[:], in_=vb[:].bitcast(BF16)[:, 0:16])
@@ -154,28 +146,47 @@ def tile_multistep_consistency_head_f7_kernel(
 
         def feature_columns():
             fb = bank("o")
-            nc.tensor.transpose(fb[:].bitcast(BF16)[:, 0:P], vecs[:], ident_b[:])
-            nc.vector.tensor_scalar(
-                out=cols[:, 0:24], in0=fb[:].bitcast(BF16)[:, 0:24], scalar1=0.25, scalar2=None, op0=ALU.mult
-            )
-            nc.vector.tensor_copy(out=cols[:, 24:48], in_=fb[:].bitcast(BF16)[:, 24:48])
-
-        def keep_gain(c):
-            nc.scalar.copy(out=gain_bc[:, c * HALF : (c + 1) * HALF], in_=gbank[c][:])
+            for c in range(3):
+                nc.tensor.transpose(
+                    fb[:].bitcast(BF16)[:, c * P : (c + 1) * P], vecs[:, c * P : (c + 1) * P], ident_b[:]
+                )
+            src = fb[:].bitcast(BF16)[:, 0 : 3 * P].rearrange("p (c r) -> p c r", c=3)
+            for c in range(3):
+                nc.vector.tensor_scalar(
+                    out=cols[:, 0:2, c::3],
+                    in0=src[:, c, 0:8].rearrange("p (v i) -> p v i", v=2),
+                    scalar1=0.25,
+                    scalar2=None,
+                    op0=ALU.mult,
+                )
+                nc.vector.tensor_copy(out=cols[:, 2:4, c::3], in_=src[:, c, 8:16].rearrange("p (v i) -> p v i", v=2))
 
         def late_coefficients():
-            nc.vector.tensor_tensor(out=gap[:], in0=sig, in1=sl[:, 8:16], op=ALU.subtract)
-            nc.vector.tensor_tensor(out=g2[:], in0=gap[:], in1=gap[:], op=ALU.mult)
-            nc.vector.scalar_tensor_tensor(
-                out=c_out[:], in0=gap[:], scalar=0.5, in1=c_in[:], op0=ALU.mult, op1=ALU.mult
-            )
-            nc.vector.tensor_scalar(out=g2[:], in0=g2[:], scalar1=0.25, scalar2=None, op0=ALU.add)
-            nc.vector.tensor_copy(out=parts[:, :, 0], in_=c_out[:])
-            nc.vector.reciprocal(out=rg[:], in_=g2[:])
-            nc.vector.tensor_tensor(out=rest[:], in0=c_out[:], in1=parts[:, :, 0], op=ALU.subtract)
-            nc.vector.tensor_scalar(out=c_skip[:], in0=rg[:], scalar1=0.25, scalar2=None, op0=ALU.mult)
-            nc.vector.tensor_copy(out=parts[:, :, 1], in_=rest[:])
-            nc.vector.tensor_tensor(out=parts[:, :, 2], in0=rest[:], in1=parts[:, :, 1], op=ALU.subtract)
+            g = nc.gpsimd
+            g.tensor_tensor(out=gap[:], in0=sig, in1=sl[:, 8:16], op=ALU.subtract)
+            g.tensor_tensor(out=g2[:], in0=gap[:], in1=gap[:], op=ALU.mult)
+            g.tensor_tensor(out=c_out[:], in0=gap[:], in1=c_in[:], op=ALU.mult)
+            g.tensor_scalar(out=g2[:], in0=g2[:], scalar1=1.0, scalar2=0.25, op0=ALU.mult, op1=ALU.add)
+            g.tensor_scalar(out=c_out[:], in0=c_out[:], scalar1=0.5, scalar2=0.0, op0=ALU.mult, op1=ALU.add)
+            g.tensor_tensor(out=rg[:], in0=g2[:], in1=mone[:], op=ALU.pow)
+            g.tensor_scalar(out=c_skip[:], in0=rg[:], scalar1=0.25, scalar2=0.0, op0=ALU.mult, op1=ALU.add)
+            g.tensor_tensor(out=ratio[:], in0=c_out[:], in1=g2[:], op=ALU.mult)
+            g.tensor_scalar(out=ratio[:], in0=ratio[:], scalar1=4.0, scalar2=0.0, op0=ALU.mult, op1=ALU.add)
+            for base, full in ((0, c_out), (4, ratio)):
+                g.tensor_copy(out=parts[:, :, base], in_=full[:])
+                g.tensor_tensor(out=rest[:], in0=full[:], in1=parts[:, :, base], op=ALU.subtract)
+                g.tensor_copy(out=parts[:, :, base + 1], in_=rest[:])
+                g.tensor_tensor(out=parts[:, :, base + 2], in0=rest[:], in1=parts[:, :, base + 1], op=ALU.subtract)
+
+        def late_loads():
+            nc.sync.dma_start(out=brows[0:4, 0, :], in_=b_out.partition_broadcast(4))
+            nc.sync.dma_start(out=brows[4:8, 1, :], in_=b_out.partition_broadcast(4))
+            for g in (1, 2):
+                load_w1(512 * g, 512)
+                load_w1(F + 512 * g, 512)
+            load_scales(w2s, w2_scales)
+            for g in range(3):
+                nc.sync.dma_start(out=w2[:, g, :], in_=w2_words[g].rearrange("p n t -> p (n t)").bitcast(I32))
 
         def make_u(rt, c, src):
             nc.vector.scalar_tensor_tensor(
@@ -186,16 +197,6 @@ def tile_multistep_consistency_head_f7_kernel(
                 op0=ALU.mult,
                 op1=ALU.mult,
             )
-
-        xc = {}
-
-        def scale_x(rt):
-            xc[rt] = work.tile([P, D], F32, align_bytes=64, name="xc", bufs=2)
-            nc.scalar.activation(out=xc[rt][:], in_=x_t[:, rt, :], func=ACT.Copy, scale=c_in[:, rt : rt + 1])
-
-        def gain_x(rt, c):
-            cs = slice(c * HALF, (c + 1) * HALF)
-            nc.gpsimd.tensor_tensor(out=u_t[:, rt, cs], in0=xc[rt][:, cs], in1=gain_bc[:, cs], op=ALU.mult)
 
         ug = {}
 
@@ -224,19 +225,31 @@ def tile_multistep_consistency_head_f7_kernel(
                     in_=ug[rt][:, g].rearrange("p r t -> p (r t)"),
                 )
 
+        cbank = []
+
         def turn_c():
             cb = bank("o")
             for rt in range(8):
                 nc.tensor.transpose(cb[:].bitcast(BF16)[:, rt * P : (rt + 1) * P], parts[:, rt, :], ident_b[:])
-            nc.scalar.copy(out=c_rows[:], in_=cb[:].bitcast(BF16))
+            cbank.append(cb)
+
+        def copy_c():
+            nc.scalar.copy(out=c_rows[:], in_=cbank[0][:].bitcast(BF16))
 
         pb = {}
 
-        def bias_mm(rt, c):
+        def bias_mm(rt, c, kind):
             pb[rt, c] = bank("o")
+            cs = slice(c * HALF, (c + 1) * HALF)
+            if kind == 1:
+                nc.tensor.matmul(pb[rt, c][:], ident_b[:], x_t[:, rt, cs], start=True, stop=False)
             nc.tensor.matmul(
-                pb[rt, c][:], c_rows[:, rt * P : (rt + 1) * P], brows[:, c * HALF : (c + 1) * HALF], start=True, stop=True
+                pb[rt, c][:], c_rows[:, rt * P : (rt + 1) * P], brows[:, kind, cs], start=(kind == 0), stop=True
             )
+
+        def scale_pre(rt, c):
+            cs = slice(c * HALF, (c + 1) * HALF)
+            nc.scalar.activation(out=pre[:, rt, cs], in_=pb[rt, c][:], func=ACT.Copy, scale=c_skip[:, rt : rt + 1])
 
         def make_pre(rt, c):
             cs = slice(c * HALF, (c + 1) * HALF)
@@ -278,7 +291,7 @@ def tile_multistep_consistency_head_f7_kernel(
             j = k % NF
             t = work.tile([P, HALF], F32, align_bytes=64, name="t", bufs=4)
             nc.scalar.activation(
-                out=t[:], in_=gate[k][:], func=ACT.Identity, scale=cols[:, j : j + 1], bias=cols[:, 12 + j : 13 + j]
+                out=t[:], in_=gate[k][:], func=ACT.Identity, scale=cols[:, 0, j : j + 1], bias=cols[:, 1, j : j + 1]
             )
             t_of[k] = t
 
@@ -296,7 +309,7 @@ def tile_multistep_consistency_head_f7_kernel(
         def op_s(k):
             j = k % NF
             s = work.tile([P, HALF], F32, align_bytes=64, name="s", bufs=4)
-            nc.scalar.activation(out=s[:], in_=z_of[k][:], func=ACT.Silu, bias=cols[:, 24 + j : 25 + j])
+            nc.scalar.activation(out=s[:], in_=z_of[k][:], func=ACT.Silu, bias=cols[:, 2, j : j + 1])
             s_of[k] = s
 
         def op_h(k):
@@ -305,7 +318,7 @@ def tile_multistep_consistency_head_f7_kernel(
             nc.vector.scalar_tensor_tensor(
                 out=h[:],
                 in0=value[k][:],
-                scalar=cols[:, 36 + j : 37 + j],
+                scalar=cols[:, 3, j : j + 1],
                 in1=s_of[k][:],
                 op0=ALU.add,
                 op1=ALU.mult,
@@ -379,13 +392,14 @@ def tile_multistep_consistency_head_f7_kernel(
             nc.gpsimd.tensor_tensor(out=o[:], in0=o1[:], in1=pre[:, rt, c * HALF : (c + 1) * HALF], op=ALU.add)
             store(rt, c, o)
 
+        EARLY = 5
+        late_coefficients()
+        late_loads()
         for rt in range(4):
             for c in range(2):
                 make_u(rt, c, gbank[c][:])
-            turn_u(rt, "og"[rt % 2])
+            turn_u(rt, "ox"[rt % 2])
             copy_u(rt)
-            if rt < 2:
-                keep_gain(rt)
         nc.scalar.activation(out=dummy[:, 1:2], in_=dummy[:, 0:1], func=ACT.Silu)
         for rt in range(4):
             quant_u(rt)
@@ -396,24 +410,18 @@ def tile_multistep_consistency_head_f7_kernel(
         def at(k, fn, *args):
             table.setdefault(k, []).append((fn, args))
 
-        for n, rt in enumerate((4, 5)):
-            at(2 * n, make_u, rt, 0, gain_bc[:, 0:HALF])
-            at(2 * n + 1, make_u, rt, 1, gain_bc[:, HALF:D])
-            at(2 * n + 2, turn_u, rt)
-            at(2 * n + 3, copy_u, rt)
-            at(2 * n + 4, quant_u, rt)
-        for n, rt in enumerate((6, 7)):
-            at(3 * n, scale_x, rt)
-            at(3 * n + 1, gain_x, rt, 0)
-            at(3 * n + 3, gain_x, rt, 1)
-            at(3 * n + 4, turn_u, rt)
-            at(3 * n + 5, copy_u, rt)
-            at(3 * n + 6, quant_u, rt)
+        for n, rt in enumerate(range(4, 8)):
+            at(n - 1, make_u, rt, 0, gbank[0][:])
+            at(n - 1, make_u, rt, 1, gbank[1][:])
+            at(2 * n + 1, turn_u, rt, "x")
+            at(2 * n + 2, copy_u, rt)
+            at(2 * n + 3, quant_u, rt)
         at(0, turn_c)
+        at(0, copy_c)
         for n in range(16):
             rt, c = divmod(n, 2)
-            at(n + 1, bias_mm, rt, c)
-            at(n + 2, make_pre, rt, c)
+            at(n + 2, bias_mm, rt, c, c)
+            at(n + 3, scale_pre if c else make_pre, rt, c)
         for q in range(5):
             s = 4 * q + 8
             at(s, weave, q, "g", 0, 128)
@@ -421,37 +429,42 @@ def tile_multistep_consistency_head_f7_kernel(
             at(s + 1, weave, q, "g", 256, 384)
             at(s + 1, weave, q, "a", 384, 512)
             at(s + 2, quant_h, q, 0, HALF)
-        for i in range(8):
-            at(18 + i, stage2, 0, i, (0, 1, 2), "o")
-            at(19 + i, finish, 0, i)
+        for i in range(EARLY):
+            at(19 + i, stage2, 0, i, (0, 1, 2), "o")
+            at(20 + i, finish, 0, i)
 
         def unit(fn, k):
             if 0 <= k < UNITS:
                 fn(k)
 
+        pe = (turn_u, turn_c, bias_mm, stage2)
         for k in range(-2, UNITS + 3):
-            unit(op_gate, k + 2)
-            unit(op_s, k - 2)
             unit(op_z, k - 1)
+            unit(op_s, k - 2)
+            for fn, args in table.get(k, []):
+                if fn in pe:
+                    fn(*args)
+            unit(op_gate, k + 2)
             unit(op_h, k - 3)
             unit(op_t, k + 1)
             unit(op_t2, k)
             unit(op_value, k - 1)
-            if k == -1:
-                late_coefficients()
             for fn, args in table.get(k, []):
-                fn(*args)
+                if fn not in pe:
+                    fn(*args)
 
-        tags = ["o", "o", "g", "g", "g", "g", "v", "v"]
+        for i in range(EARLY, 8):
+            stage2(0, i, (0, 1, 2), "oox"[i % 3])
+            finish(0, i)
+        tags = ["g", "g", "g", "v", "v", "o", "o", "x"]
         for i in range(8):
             stage2(1, i, (0, 1), tags[i])
-        weave(5, "v", 0, 128)
-        weave(5, "a", 128, 256)
-        weave(5, "g", 256, 384)
-        quant_h(5, 0, 128)
-        weave(5, "v", 384, 512)
-        for r in range(1, 4):
-            quant_h(5, 128 * r, 128 * (r + 1))
+        for r in range(4):
+            weave(5, "va"[r % 2], 128 * r, 128 * (r + 1))
+            if r != 1:
+                quant_h(5, 128 * r, 128 * (r + 1))
+            if r == 2:
+                quant_h(5, 128, 256)
         for i in range(8):
             stage2(1, i, (2,))
             if i % 3 == 1:

@@ -18,7 +18,7 @@ P = 128
 HALF = 512
 NF = F // P
 
-UNITS = 2 * NF
+S = {"ga":[5],"u":[-1,-2,3,4],"turn":[1,2,5,8],"tc":[1,4,5,9],"qu":9,"pre":[1,1,6,3,4,7,8,9,12,11,13,14,15,16,17,18],"kind":[0,1,0,1,0,0,0,1,0,1,1,1,0,0,1,1],"weave":[[10,9],[13,14],[17,16],[25,23],[25,25]],"weng":["ag","gv","ag","ga","ag","vgvv"],"qh":[11,15,17,28,28],"early":3,"s2":[24,19,23],"fag0":[3,4],"fag":[4],"qord":[2,0,3,1],"split":0,"tags":["g","v","g","v","o","o","g","x"]}
 FLOPS = 2 * M * D * 2 * F + 2 * M * F * D
 
 
@@ -43,7 +43,6 @@ def tile_multistep_consistency_head_f7_kernel(
         ident = keep.tile([P, P], F32, align_bytes=64, name="ident")
         ident_b = keep.tile([P, P], BF16, align_bytes=64, name="ident_b")
         x_t = keep.tile([P, 8, D], BF16, align_bytes=64, name="x_t")
-        u_t = keep.tile([P, 8, D], BF16, align_bytes=64, name="u_t")
         pre = keep.tile([P, 8, D], F32, align_bytes=64, name="pre")
         w1 = keep.tile([P, 2, 4 * F], U8, align_bytes=64, name="w1")
         w1s = keep.tile([P, 2, 2 * F], U8, align_bytes=64, name="w1s")
@@ -57,9 +56,11 @@ def tile_multistep_consistency_head_f7_kernel(
         cols = keep.tile([P, 4, NF], F32, align_bytes=64, name="cols")
         sig_b = keep.tile([P, 8], BF16, align_bytes=64, name="sig_b")
         cn = keep.tile([P, M], F32, align_bytes=64, name="cn")
+        gain_bc = keep.tile([P, D], BF16, align_bytes=64, name="gain_bc")
         parts = keep.tile([P, 8, P], BF16, align_bytes=64, name="parts")
         rest = keep.tile([P, 8], F32, name="rest")
         ratio = keep.tile([P, 8], F32, name="ratio")
+        rest2 = keep.tile([P, 8], F32, name="rest2")
         c_rows = keep.tile([P, 8 * P], BF16, align_bytes=64, name="c_rows")
         dummy = keep.tile([P, 2], F32, align_bytes=64, name="dummy")
         gap = keep.tile([P, 8], F32, name="gap")
@@ -114,20 +115,19 @@ def tile_multistep_consistency_head_f7_kernel(
         load_x(0, 1)
         load_x(1, 1)
         load_x(2, 2)
+        load_x(4, 2)
         load_scales(w1s, w1_scales)
         for v, vec in enumerate((e_mul, e_add, b_gate, b_value)):
             nc.sync.dma_start(out=vecs[4 * v : 4 * v + 4, :], in_=vec.rearrange("(j p) -> j p", j=4))
         load_w1(0, 512)
         load_w1(F, 512)
-        load_x(4, 2)
         load_x(6, 2)
         vb = bank("o")
         nc.tensor.transpose(vb[:].bitcast(BF16)[:, 0:P], sv[:], ident_b[:])
-        nc.vector.tensor_copy(out=sl[:], in_=vb[:].bitcast(BF16)[:, 0:16])
-        sig = sl[:, 0:8]
-        nc.vector.tensor_tensor(out=s2[:], in0=sig, in1=sig, op=ALU.mult)
+        nc.vector.tensor_scalar(out=sl[:], in0=vb[:].bitcast(BF16)[:, 0:16], scalar1=0.5, scalar2=None, op0=ALU.mult)
+        nc.vector.tensor_tensor(out=s2[:], in0=sl[:, 0:8], in1=sl[:, 0:8], op=ALU.mult)
         nc.vector.tensor_copy(out=sig_b[:], in_=vb[:].bitcast(BF16)[:, 0:8])
-        nc.vector.tensor_scalar(out=s2[:], in0=s2[:], scalar1=0.25, scalar2=None, op0=ALU.add)
+        nc.vector.tensor_scalar(out=s2[:], in0=s2[:], scalar1=4.0, scalar2=0.25, op0=ALU.mult, op1=ALU.add)
         nc.gpsimd.tensor_tensor(out=c_in[:], in0=s2[:], in1=mhalf[:], op=ALU.pow)
         gbank = [bank("v"), bank("v")]
         for c in range(2):
@@ -141,6 +141,8 @@ def tile_multistep_consistency_head_f7_kernel(
                 start=True,
                 stop=True,
             )
+        for c in range(2):
+            nc.scalar.copy(out=gain_bc[:, c * HALF : (c + 1) * HALF], in_=gbank[c][:])
         for c in range(2):
             nc.scalar.activation(out=cn[:, c * HALF : (c + 1) * HALF], in_=sbank[c][:], func=ACT.Ln)
 
@@ -163,20 +165,20 @@ def tile_multistep_consistency_head_f7_kernel(
 
         def late_coefficients():
             g = nc.gpsimd
-            g.tensor_tensor(out=gap[:], in0=sig, in1=sl[:, 8:16], op=ALU.subtract)
+            g.tensor_tensor(out=gap[:], in0=sl[:, 0:8], in1=sl[:, 8:16], op=ALU.subtract)
             g.tensor_tensor(out=g2[:], in0=gap[:], in1=gap[:], op=ALU.mult)
             g.tensor_tensor(out=c_out[:], in0=gap[:], in1=c_in[:], op=ALU.mult)
-            g.tensor_scalar(out=g2[:], in0=g2[:], scalar1=1.0, scalar2=0.25, op0=ALU.mult, op1=ALU.add)
-            g.tensor_scalar(out=c_out[:], in0=c_out[:], scalar1=0.5, scalar2=0.0, op0=ALU.mult, op1=ALU.add)
-            g.tensor_tensor(out=rg[:], in0=g2[:], in1=mone[:], op=ALU.pow)
-            g.tensor_scalar(out=c_skip[:], in0=rg[:], scalar1=0.25, scalar2=0.0, op0=ALU.mult, op1=ALU.add)
+            g.tensor_scalar(out=g2[:], in0=g2[:], scalar1=16.0, scalar2=1.0, op0=ALU.mult, op1=ALU.add)
+            g.tensor_copy(out=parts[:, :, 0], in_=c_out[:])
             g.tensor_tensor(out=ratio[:], in0=c_out[:], in1=g2[:], op=ALU.mult)
-            g.tensor_scalar(out=ratio[:], in0=ratio[:], scalar1=4.0, scalar2=0.0, op0=ALU.mult, op1=ALU.add)
-            for base, full in ((0, c_out), (4, ratio)):
-                g.tensor_copy(out=parts[:, :, base], in_=full[:])
-                g.tensor_tensor(out=rest[:], in0=full[:], in1=parts[:, :, base], op=ALU.subtract)
-                g.tensor_copy(out=parts[:, :, base + 1], in_=rest[:])
-                g.tensor_tensor(out=parts[:, :, base + 2], in0=rest[:], in1=parts[:, :, base + 1], op=ALU.subtract)
+            g.tensor_tensor(out=c_skip[:], in0=g2[:], in1=mone[:], op=ALU.pow)
+            g.tensor_tensor(out=rest[:], in0=c_out[:], in1=parts[:, :, 0], op=ALU.subtract)
+            g.tensor_copy(out=parts[:, :, 4], in_=ratio[:])
+            g.tensor_copy(out=parts[:, :, 1], in_=rest[:])
+            g.tensor_tensor(out=rest2[:], in0=ratio[:], in1=parts[:, :, 4], op=ALU.subtract)
+            g.tensor_tensor(out=parts[:, :, 2], in0=rest[:], in1=parts[:, :, 1], op=ALU.subtract)
+            g.tensor_copy(out=parts[:, :, 5], in_=rest2[:])
+            g.tensor_tensor(out=parts[:, :, 6], in0=rest2[:], in1=parts[:, :, 5], op=ALU.subtract)
 
         def late_loads():
             nc.sync.dma_start(out=brows[0:4, 0, :], in_=b_out.partition_broadcast(4))
@@ -188,9 +190,16 @@ def tile_multistep_consistency_head_f7_kernel(
             for g in range(3):
                 nc.sync.dma_start(out=w2[:, g, :], in_=w2_words[g].rearrange("p n t -> p (n t)").bitcast(I32))
 
+        u_of = {}
+
+        def u_tile(rt):
+            if rt not in u_of:
+                u_of[rt] = work.tile([P, D], BF16, align_bytes=64, name="u", bufs=4)
+            return u_of[rt]
+
         def make_u(rt, c, src):
             nc.vector.scalar_tensor_tensor(
-                out=u_t[:, rt, c * HALF : (c + 1) * HALF],
+                out=u_tile(rt)[:, c * HALF : (c + 1) * HALF],
                 in0=x_t[:, rt, c * HALF : (c + 1) * HALF],
                 scalar=c_in[:, rt : rt + 1],
                 in1=src,
@@ -198,11 +207,30 @@ def tile_multistep_consistency_head_f7_kernel(
                 op1=ALU.mult,
             )
 
-        ug = {}
+        def make_u_late(rt):
+            nc.vector.scalar_tensor_tensor(
+                out=u_tile(rt)[:],
+                in0=x_t[:, rt, :],
+                scalar=c_in[:, rt : rt + 1],
+                in1=gain_bc[:],
+                op0=ALU.mult,
+                op1=ALU.mult,
+            )
+
+        xg = {}
+
+        def gain_x(rt):
+            xg[rt] = work.tile([P, D], F32, align_bytes=64, name="xg", bufs=1)
+            nc.gpsimd.tensor_tensor(out=xg[rt][:], in0=x_t[:, rt, :], in1=gain_bc[:], op=ALU.mult)
+
+        def scale_u(rt):
+            nc.scalar.activation(out=u_tile(rt)[:], in_=xg[rt][:], func=ACT.Copy, scale=c_in[:, rt : rt + 1])
+
+        ug, grouped = {}, {}
 
         def turn_u(rt, tag="o"):
             xb = bank(tag)
-            words = u_t[:, rt, :].bitcast(F32)
+            words = u_of[rt][:].bitcast(F32)
             for g in range(2):
                 for u in range(2):
                     i = 2 * g + u
@@ -210,20 +238,21 @@ def tile_multistep_consistency_head_f7_kernel(
             ug[rt] = xb
 
         def copy_u(rt):
-            grouped = work.tile([P, 2, P, 4], BF16, align_bytes=64, name="ug")
+            hb, r = divmod(rt, 4)
+            if r == 0:
+                grouped[hb] = work.tile([P, 2, HALF, 4], BF16, align_bytes=64, name="ug", bufs=2)
             nc.scalar.copy(
-                out=grouped[:].bitcast(F32),
+                out=grouped[hb][:, :, r * P : (r + 1) * P, :].bitcast(F32),
                 in_=ug[rt][:].rearrange("p (g u r) -> p g r u", g=2, u=2),
             )
-            ug[rt] = grouped
 
-        def quant_u(rt):
-            for g in range(2):
-                nc.vector.quantize_mx(
-                    out=u_codes[:, g, rt * P : (rt + 1) * P].bitcast(FP8X4),
-                    scales=u_scales[:, g, rt * P : (rt + 1) * P],
-                    in_=ug[rt][:, g].rearrange("p r t -> p (r t)"),
-                )
+        def quant_u(hb, g, r0, r1):
+            c0 = hb * HALF
+            nc.vector.quantize_mx(
+                out=u_codes[:, g, c0 + r0 : c0 + r1].bitcast(FP8X4),
+                scales=u_scales[:, g, c0 + r0 : c0 + r1],
+                in_=grouped[hb][:, g, r0:r1, :].rearrange("p r t -> p (r t)"),
+            )
 
         cbank = []
 
@@ -263,23 +292,30 @@ def tile_multistep_consistency_head_f7_kernel(
             )
 
         def stage1(k, col0, tag):
-            hb, j = divmod(k, NF)
+            hb, j, r0, n = units[k]
+            r0 += hb * HALF
             b = bank(tag)
             c0 = col0 + P * j
             for g in range(2):
                 nc.tensor.matmul_mx(
-                    out=b[:],
+                    out=b[:, 0:n],
                     lhsT=w1[:, g, 2 * c0 : 2 * (c0 + P)].bitcast(FP4X4),
                     lhsT_scale=w1s[:, g, c0 : c0 + P],
-                    rhs=u_codes[:, g, hb * HALF : (hb + 1) * HALF].bitcast(FP8X4),
-                    rhs_scale=u_scales[:, g, hb * HALF : (hb + 1) * HALF],
+                    rhs=u_codes[:, g, r0 : r0 + n].bitcast(FP8X4),
+                    rhs_scale=u_scales[:, g, r0 : r0 + n],
                     start=(g == 0),
                     stop=(g == 1),
                 )
             return b
 
+        units = [(0, j, 0, HALF) for j in range(NF)] + [(1, j, 0, HALF) for j in range(8)]
+        if S["split"]:
+            units += [(1, j, r0, 256) for r0 in (0, 256) for j in range(8, NF)]
+        else:
+            units += [(1, j, 0, HALF) for j in range(8, NF)]
+        UNITS = len(units)
         gate, value, t_of, z_of, s_of = {}, {}, {}, {}, {}
-        hd, hg = {}, {}
+        hd, hg, h_of = {}, {}, {}
 
         def op_gate(k):
             gate[k] = stage1(k, 0, "g")
@@ -288,52 +324,54 @@ def tile_multistep_consistency_head_f7_kernel(
             value[k] = stage1(k, F, "v")
 
         def op_t(k):
-            j = k % NF
+            hb, j, r0, n = units[k]
             t = work.tile([P, HALF], F32, align_bytes=64, name="t", bufs=4)
             nc.scalar.activation(
-                out=t[:], in_=gate[k][:], func=ACT.Identity, scale=cols[:, 0, j : j + 1], bias=cols[:, 1, j : j + 1]
+                out=t[:, 0:n], in_=gate[k][:, 0:n], func=ACT.Identity, scale=cols[:, 0, j : j + 1], bias=cols[:, 1, j : j + 1]
             )
             t_of[k] = t
 
         def op_t2(k):
-            hb = k // NF
+            hb, j, r0, n = units[k]
+            r0 += hb * HALF
             t2 = work.tile([P, HALF], F32, align_bytes=64, name="t2", bufs=4)
-            nc.gpsimd.tensor_tensor(out=t2[:], in0=t_of[k][:], in1=cn[:, hb * HALF : (hb + 1) * HALF], op=ALU.mult)
+            nc.gpsimd.tensor_tensor(out=t2[:, 0:n], in0=t_of[k][:, 0:n], in1=cn[:, r0 : r0 + n], op=ALU.mult)
             t_of[k] = t2
 
         def op_z(k):
             z = work.tile([P, HALF], F32, align_bytes=64, name="z", bufs=4)
-            nc.vector.tensor_tensor(out=z[:], in0=gate[k][:], in1=t_of[k][:], op=ALU.add)
+            n = units[k][3]
+            nc.vector.tensor_tensor(out=z[:, 0:n], in0=gate[k][:, 0:n], in1=t_of[k][:, 0:n], op=ALU.add)
             z_of[k] = z
 
         def op_s(k):
-            j = k % NF
+            hb, j, r0, n = units[k]
             s = work.tile([P, HALF], F32, align_bytes=64, name="s", bufs=4)
-            nc.scalar.activation(out=s[:], in_=z_of[k][:], func=ACT.Silu, bias=cols[:, 2, j : j + 1])
+            nc.scalar.activation(out=s[:, 0:n], in_=z_of[k][:, 0:n], func=ACT.Silu, bias=cols[:, 2, j : j + 1])
             s_of[k] = s
 
         def op_h(k):
-            j = k % NF
+            hb, j, r0, n = units[k]
             h = work.tile([P, HALF], BF16, align_bytes=64, name="h", bufs=6)
             nc.vector.scalar_tensor_tensor(
-                out=h[:],
-                in0=value[k][:],
+                out=h[:, 0:n],
+                in0=value[k][:, 0:n],
                 scalar=cols[:, 3, j : j + 1],
-                in1=s_of[k][:],
+                in1=s_of[k][:, 0:n],
                 op0=ALU.add,
                 op1=ALU.mult,
             )
-            q, jj = divmod(k, 4)
-            if jj == 0:
-                hd[q] = work.tile([P, 4, HALF], BF16, align_bytes=64, name="hd")
+            g, jj = divmod(j, 4)
+            if (hb, g) not in hd:
+                hd[hb, g] = work.tile([P, 4, HALF], BF16, align_bytes=64, name="hd")
             for t in range(4):
-                nc.sync.dma_start(out=hd[q][32 * jj : 32 * jj + 32, t, :], in_=h[t:P:4, :])
+                nc.sync.dma_start(out=hd[hb, g][32 * jj : 32 * jj + 32, t, r0 : r0 + n], in_=h[t:P:4, 0:n])
 
         def weave(q, eng, r0, r1):
             if q not in hg:
                 hg[q] = work.tile([P, HALF, 4], BF16, align_bytes=64, name="hg")
             dst = hg[q][:, r0:r1, :]
-            src = hd[q][:, :, r0:r1].rearrange("p t r -> p r t")
+            src = hd[divmod(q, 3)][:, :, r0:r1].rearrange("p t r -> p r t")
             if eng == "g":
                 nc.gpsimd.tensor_scalar(out=dst, in0=src, scalar1=1.0, scalar2=0.0, op0=ALU.mult, op1=ALU.add)
             elif eng == "a":
@@ -392,18 +430,20 @@ def tile_multistep_consistency_head_f7_kernel(
             nc.gpsimd.tensor_tensor(out=o[:], in0=o1[:], in1=pre[:, rt, c * HALF : (c + 1) * HALF], op=ALU.add)
             store(rt, c, o)
 
-        EARLY = 5
         late_coefficients()
+        for rt in S["ga"]:
+            gain_x(rt)
         late_loads()
         for rt in range(4):
             for c in range(2):
                 make_u(rt, c, gbank[c][:])
             turn_u(rt, "ox"[rt % 2])
             copy_u(rt)
-        nc.scalar.activation(out=dummy[:, 1:2], in_=dummy[:, 0:1], func=ACT.Silu)
-        for rt in range(4):
-            quant_u(rt)
+        for r in range(2):
+            for g in range(2):
+                quant_u(0, g, 2 * P * r, 2 * P * (r + 1))
         feature_columns()
+        nc.scalar.activation(out=dummy[:, 1:2], in_=dummy[:, 0:1], func=ACT.Silu)
 
         table = {}
 
@@ -411,34 +451,43 @@ def tile_multistep_consistency_head_f7_kernel(
             table.setdefault(k, []).append((fn, args))
 
         for n, rt in enumerate(range(4, 8)):
-            at(n - 1, make_u, rt, 0, gbank[0][:])
-            at(n - 1, make_u, rt, 1, gbank[1][:])
-            at(2 * n + 1, turn_u, rt, "x")
-            at(2 * n + 2, copy_u, rt)
-            at(2 * n + 3, quant_u, rt)
+            if rt in S["ga"]:
+                at(S["u"][n], scale_u, rt)
+            else:
+                at(S["u"][n], make_u_late, rt)
+            at(S["turn"][n], turn_u, rt, "x")
+            at(S["tc"][n], copy_u, rt)
+        at(S["qu"], quant_u, 1, 0, 0, HALF)
+        at(S["qu"], quant_u, 1, 1, 0, HALF)
         at(0, turn_c)
         at(0, copy_c)
         for n in range(16):
             rt, c = divmod(n, 2)
-            at(n + 2, bias_mm, rt, c, c)
-            at(n + 3, scale_pre if c else make_pre, rt, c)
+            kind = S["kind"][n]
+            at(S["pre"][n], bias_mm, rt, c, kind)
+            at(S["pre"][n] + 1, scale_pre if kind else make_pre, rt, c)
         for q in range(5):
-            s = 4 * q + 8
-            at(s, weave, q, "g", 0, 128)
-            at(s, weave, q, "a", 128, 256)
-            at(s + 1, weave, q, "g", 256, 384)
-            at(s + 1, weave, q, "a", 384, 512)
-            at(s + 2, quant_h, q, 0, HALF)
-        for i in range(EARLY):
-            at(19 + i, stage2, 0, i, (0, 1, 2), "o")
-            at(20 + i, finish, 0, i)
+            w = HALF // len(S["weave"][q])
+            for n, k in enumerate(S["weave"][q]):
+                at(k, weave, q, S["weng"][q][n], w * n, w * n + w)
+            at(S["qh"][q], quant_h, q, 0, HALF)
+        if S["split"]:
+            for r in range(2):
+                at(S["w5"][r], weave, 5, S["weng"][5][r], 128 * r, 128 * (r + 1))
+                at(S["q5"][r], quant_h, 5, 128 * r, 128 * (r + 1))
+            for i in range(4):
+                at(S["s5"][i], stage2, 1, i, (0, 1, 2), "oxo"[i % 3])
+                at(S["s5"][i] + 1, finish_ag if i in S["fag"] else finish, 1, i)
+        for i in range(S["early"]):
+            at(S["s2"][i], stage2, 0, i, (0, 1, 2), "o")
+            at(S["s2"][i] + 1, finish_ag if i in S["fag0"] else finish, 0, i)
 
         def unit(fn, k):
             if 0 <= k < UNITS:
                 fn(k)
 
         pe = (turn_u, turn_c, bias_mm, stage2)
-        for k in range(-2, UNITS + 3):
+        for k in range(-2, UNITS + 5):
             unit(op_z, k - 1)
             unit(op_s, k - 2)
             for fn, args in table.get(k, []):
@@ -453,21 +502,16 @@ def tile_multistep_consistency_head_f7_kernel(
                 if fn not in pe:
                     fn(*args)
 
-        for i in range(EARLY, 8):
+        for i in range(S["early"], 8):
             stage2(0, i, (0, 1, 2), "oox"[i % 3])
-            finish(0, i)
-        tags = ["g", "g", "g", "v", "v", "o", "o", "x"]
-        for i in range(8):
-            stage2(1, i, (0, 1), tags[i])
-        for r in range(4):
-            weave(5, "va"[r % 2], 128 * r, 128 * (r + 1))
-            if r != 1:
-                quant_h(5, 128 * r, 128 * (r + 1))
-            if r == 2:
-                quant_h(5, 128, 256)
-        for i in range(8):
+            (finish_ag if i in S["fag0"] else finish)(0, i)
+        first = 4 if S["split"] else 0
+        for i in range(first, 8):
+            stage2(1, i, (0, 1), S["tags"][i])
+        for r in range(first // 2, 4):
+            weave(5, S["weng"][5][r], 128 * r, 128 * (r + 1))
+        for r in range(first // 2, 4):
+            quant_h(5, 128 * r, 128 * (r + 1))
+        for i in range(first, 8):
             stage2(1, i, (2,))
-            if i % 3 == 1:
-                finish_ag(1, i)
-            else:
-                finish(1, i)
+            (finish_ag if i in S["fag"] else finish)(1, i)

from contextlib import ExitStack

import concourse.mybir as mybir
from concourse.masks import make_identity

F32 = mybir.dt.float32
BF16 = mybir.dt.bfloat16
U32 = mybir.dt.uint32
I32 = mybir.dt.int32
U8 = mybir.dt.uint8
FP8X4 = mybir.dt.float8_e4m3fn_x4
FP4X4 = mybir.dt.float4_e2m1fn_x4
ALU = mybir.AluOpType
ACT = mybir.ActivationFunctionType

M, D, F = 1024, 1024, 1536
P = 128
HALF = 512
NF = F // P

S = {"ga":[5],"u":[-1,-2,3,4],"turn":[1,2,5,8],"tc":[1,4,5,9],"qu":9,"pre":[1,1,6,3,4,7,8,9,12,11,13,14,15,16,17,18],"kind":[0,1,0,1,0,0,0,1,0,1,1,1,0,0,1,1],"weave":[[10,9],[13,14],[17,16],[25,23],[25,25]],"weng":["ag","gv","ag","ga","ag","vgvv"],"qh":[11,15,17,28,28],"early":3,"s2":[24,19,23],"fag0":[3,4],"fag":[4],"qord":[2,0,3,1],"split":0,"tags":["g","v","g","v","o","o","g","x"]}
FLOPS = 2 * M * D * 2 * F + 2 * M * F * D


def tile_multistep_consistency_head_f7_kernel(
    tc, x, sigma, sigma_lo, in_gain, w1_words, w1_scales, e_mul, e_add, b_gate, b_value, w2_words, w2_scales, b_out, out
):
    nc = tc.nc
    with ExitStack() as ctx:
        keep = ctx.enter_context(tc.tile_pool(name="keep", bufs=1))
        work = ctx.enter_context(tc.tile_pool(name="work", bufs=3))
        ps = ctx.enter_context(tc.psum_pool(name="ps", bufs=1))
        ctx.enter_context(tc.manual_schedule())

        def bank(tag):
            return ps.tile([P, HALF], F32, tag=tag, bufs={"g": 3, "v": 2, "o": 2, "x": 1}[tag], name="bank_" + tag)

        vecs = keep.tile([P, 3 * P], BF16, align_bytes=64, name="vecs")
        sv = keep.tile([P, P], BF16, align_bytes=64, name="sv")
        gb = keep.tile([P, D], BF16, align_bytes=64, name="gb")
        brows = keep.tile([P, 2, D], BF16, align_bytes=64, name="brows")
        ones = keep.tile([P, P], BF16, align_bytes=64, name="ones")
        ident = keep.tile([P, P], F32, align_bytes=64, name="ident")
        ident_b = keep.tile([P, P], BF16, align_bytes=64, name="ident_b")
        x_t = keep.tile([P, 8, D], BF16, align_bytes=64, name="x_t")
        pre = keep.tile([P, 8, D], F32, align_bytes=64, name="pre")
        w1 = keep.tile([P, 2, 4 * F], U8, align_bytes=64, name="w1")
        w1s = keep.tile([P, 2, 2 * F], U8, align_bytes=64, name="w1s")
        w2 = keep.tile([P, 3, D], I32, align_bytes=64, name="w2")
        w2s = keep.tile([P, 3, D], U8, align_bytes=64, name="w2s")
        u_codes = keep.tile([P, 2, M], U32, align_bytes=64, name="u_codes")
        u_scales = keep.tile([P, 2, M], U8, align_bytes=64, name="u_scales")
        h_codes = keep.tile([P, 2, 3, HALF], U32, align_bytes=64, name="h_codes")
        h_scales = keep.tile([P, 2, 3, HALF], U8, align_bytes=64, name="h_scales")
        sl = keep.tile([P, 16], F32, align_bytes=64, name="sl")
        cols = keep.tile([P, 4, NF], F32, align_bytes=64, name="cols")
        sig_b = keep.tile([P, 8], BF16, align_bytes=64, name="sig_b")
        cn = keep.tile([P, M], F32, align_bytes=64, name="cn")
        gain_bc = keep.tile([P, D], BF16, align_bytes=64, name="gain_bc")
        parts = keep.tile([P, 8, P], BF16, align_bytes=64, name="parts")
        rest = keep.tile([P, 8], F32, name="rest")
        ratio = keep.tile([P, 8], F32, name="ratio")
        rest2 = keep.tile([P, 8], F32, name="rest2")
        c_rows = keep.tile([P, 8 * P], BF16, align_bytes=64, name="c_rows")
        dummy = keep.tile([P, 2], F32, align_bytes=64, name="dummy")
        gap = keep.tile([P, 8], F32, name="gap")
        s2 = keep.tile([P, 8], F32, name="s2")
        g2 = keep.tile([P, 8], F32, name="g2")
        rg = keep.tile([P, 8], F32, name="rg")
        c_in = keep.tile([P, 8], F32, name="c_in")
        c_skip = keep.tile([P, 8], F32, name="c_skip")
        c_out = keep.tile([P, 8], F32, name="c_out")
        mhalf = keep.tile([P, 8], F32, name="mhalf")
        mone = keep.tile([P, 8], F32, name="mone")

        make_identity(nc, ident[:])
        nc.vector.memset(sv[:], 0.0)
        nc.vector.memset(gb[:], 0.0)
        nc.vector.memset(dummy[:], 1.0)
        nc.vector.memset(ones[:], 1.0)
        nc.vector.memset(vecs[:], 0.0)
        nc.vector.memset(w1s[:].bitcast(I32), 0)
        nc.vector.memset(parts[:].bitcast(I32), 0)
        nc.vector.memset(brows[:].bitcast(I32), 0)
        nc.vector.memset(w2s[:].bitcast(I32), 0)
        nc.gpsimd.memset(mhalf[:], -0.5)
        nc.gpsimd.memset(mone[:], -1.0)
        nc.scalar.copy(out=ident_b[:], in_=ident[:])
        nc.scalar.activation(out=dummy[:, 1:2], in_=dummy[:, 0:1], func=ACT.Ln)

        def load_vec(t, v, row, n):
            nc.sync.dma_start(out=t[row : row + n, :], in_=v.rearrange("(j p) -> j p", p=P))

        def load_x(r0, n):
            nc.sync.dma_start(
                out=x_t[:, r0 : r0 + n, :], in_=x[r0 * P : (r0 + n) * P, :].rearrange("(n p) d -> p n d", p=P)
            )

        def load_w1(c0, n):
            nc.sync.dma_start(
                out=w1[:, :, 2 * c0 : 2 * (c0 + n)].bitcast(I32),
                in_=w1_words[:, :, 2 * c0 : 2 * (c0 + n)].rearrange("g p b -> p g b").bitcast(I32),
            )

        def load_scales(plane, scales):
            for q in range(4):
                nc.sync.dma_start(
                    out=plane[32 * q : 32 * q + 4, :, :].bitcast(I32),
                    in_=scales[:, 4 * q : 4 * q + 4, :].rearrange("g q n -> q g n").bitcast(I32),
                )

        load_vec(sv, sigma, 0, 8)
        load_vec(sv, sigma_lo, 8, 8)
        nc.sync.dma_start(out=gb[0:1, :], in_=in_gain.unsqueeze(0))
        load_x(0, 1)
        load_x(1, 1)
        load_x(2, 2)
        load_x(4, 2)
        load_scales(w1s, w1_scales)
        for v, vec in enumerate((e_mul, e_add, b_gate, b_value)):
            nc.sync.dma_start(out=vecs[4 * v : 4 * v + 4, :], in_=vec.rearrange("(j p) -> j p", j=4))
        load_w1(0, 512)
        load_w1(F, 512)
        load_x(6, 2)
        vb = bank("o")
        nc.tensor.transpose(vb[:].bitcast(BF16)[:, 0:P], sv[:], ident_b[:])
        nc.vector.tensor_scalar(out=sl[:], in0=vb[:].bitcast(BF16)[:, 0:16], scalar1=0.5, scalar2=None, op0=ALU.mult)
        nc.vector.tensor_tensor(out=s2[:], in0=sl[:, 0:8], in1=sl[:, 0:8], op=ALU.mult)
        nc.vector.tensor_copy(out=sig_b[:], in_=vb[:].bitcast(BF16)[:, 0:8])
        nc.vector.tensor_scalar(out=s2[:], in0=s2[:], scalar1=4.0, scalar2=0.25, op0=ALU.mult, op1=ALU.add)
        nc.gpsimd.tensor_tensor(out=c_in[:], in0=s2[:], in1=mhalf[:], op=ALU.pow)
        gbank = [bank("v"), bank("v")]
        for c in range(2):
            nc.tensor.matmul(gbank[c][:], ones[:], gb[:, c * HALF : (c + 1) * HALF], start=True, stop=True)
        sbank = [bank("g"), bank("g")]
        for rt in range(8):
            nc.tensor.matmul(
                sbank[rt // 4][:, (rt % 4) * P : (rt % 4 + 1) * P],
                sig_b[:, rt : rt + 1].to_broadcast([P, P]),
                ident_b[:],
                start=True,
                stop=True,
            )
        for c in range(2):
            nc.scalar.copy(out=gain_bc[:, c * HALF : (c + 1) * HALF], in_=gbank[c][:])
        for c in range(2):
            nc.scalar.activation(out=cn[:, c * HALF : (c + 1) * HALF], in_=sbank[c][:], func=ACT.Ln)

        def feature_columns():
            fb = bank("o")
            for c in range(3):
                nc.tensor.transpose(
                    fb[:].bitcast(BF16)[:, c * P : (c + 1) * P], vecs[:, c * P : (c + 1) * P], ident_b[:]
                )
            src = fb[:].bitcast(BF16)[:, 0 : 3 * P].rearrange("p (c r) -> p c r", c=3)
            for c in range(3):
                nc.vector.tensor_scalar(
                    out=cols[:, 0:2, c::3],
                    in0=src[:, c, 0:8].rearrange("p (v i) -> p v i", v=2),
                    scalar1=0.25,
                    scalar2=None,
                    op0=ALU.mult,
                )
                nc.vector.tensor_copy(out=cols[:, 2:4, c::3], in_=src[:, c, 8:16].rearrange("p (v i) -> p v i", v=2))

        def late_coefficients():
            g = nc.gpsimd
            g.tensor_tensor(out=gap[:], in0=sl[:, 0:8], in1=sl[:, 8:16], op=ALU.subtract)
            g.tensor_tensor(out=g2[:], in0=gap[:], in1=gap[:], op=ALU.mult)
            g.tensor_tensor(out=c_out[:], in0=gap[:], in1=c_in[:], op=ALU.mult)
            g.tensor_scalar(out=g2[:], in0=g2[:], scalar1=16.0, scalar2=1.0, op0=ALU.mult, op1=ALU.add)
            g.tensor_copy(out=parts[:, :, 0], in_=c_out[:])
            g.tensor_tensor(out=ratio[:], in0=c_out[:], in1=g2[:], op=ALU.mult)
            g.tensor_tensor(out=c_skip[:], in0=g2[:], in1=mone[:], op=ALU.pow)
            g.tensor_tensor(out=rest[:], in0=c_out[:], in1=parts[:, :, 0], op=ALU.subtract)
            g.tensor_copy(out=parts[:, :, 4], in_=ratio[:])
            g.tensor_copy(out=parts[:, :, 1], in_=rest[:])
            g.tensor_tensor(out=rest2[:], in0=ratio[:], in1=parts[:, :, 4], op=ALU.subtract)
            g.tensor_tensor(out=parts[:, :, 2], in0=rest[:], in1=parts[:, :, 1], op=ALU.subtract)
            g.tensor_copy(out=parts[:, :, 5], in_=rest2[:])
            g.tensor_tensor(out=parts[:, :, 6], in0=rest2[:], in1=parts[:, :, 5], op=ALU.subtract)

        def late_loads():
            nc.sync.dma_start(out=brows[0:4, 0, :], in_=b_out.partition_broadcast(4))
            nc.sync.dma_start(out=brows[4:8, 1, :], in_=b_out.partition_broadcast(4))
            for g in (1, 2):
                load_w1(512 * g, 512)
                load_w1(F + 512 * g, 512)
            load_scales(w2s, w2_scales)
            for g in range(3):
                nc.sync.dma_start(out=w2[:, g, :], in_=w2_words[g].rearrange("p n t -> p (n t)").bitcast(I32))

        u_of = {}

        def u_tile(rt):
            if rt not in u_of:
                u_of[rt] = work.tile([P, D], BF16, align_bytes=64, name="u", bufs=4)
            return u_of[rt]

        def make_u(rt, c, src):
            nc.vector.scalar_tensor_tensor(
                out=u_tile(rt)[:, c * HALF : (c + 1) * HALF],
                in0=x_t[:, rt, c * HALF : (c + 1) * HALF],
                scalar=c_in[:, rt : rt + 1],
                in1=src,
                op0=ALU.mult,
                op1=ALU.mult,
            )

        def make_u_late(rt):
            nc.vector.scalar_tensor_tensor(
                out=u_tile(rt)[:],
                in0=x_t[:, rt, :],
                scalar=c_in[:, rt : rt + 1],
                in1=gain_bc[:],
                op0=ALU.mult,
                op1=ALU.mult,
            )

        xg = {}

        def gain_x(rt):
            xg[rt] = work.tile([P, D], F32, align_bytes=64, name="xg", bufs=1)
            nc.gpsimd.tensor_tensor(out=xg[rt][:], in0=x_t[:, rt, :], in1=gain_bc[:], op=ALU.mult)

        def scale_u(rt):
            nc.scalar.activation(out=u_tile(rt)[:], in_=xg[rt][:], func=ACT.Copy, scale=c_in[:, rt : rt + 1])

        ug, grouped = {}, {}

        def turn_u(rt, tag="o"):
            xb = bank(tag)
            words = u_of[rt][:].bitcast(F32)
            for g in range(2):
                for u in range(2):
                    i = 2 * g + u
                    nc.tensor.transpose(xb[:, i * P : (i + 1) * P], words[:, 256 * g + u : 256 * (g + 1) : 2], ident[:])
            ug[rt] = xb

        def copy_u(rt):
            hb, r = divmod(rt, 4)
            if r == 0:
                grouped[hb] = work.tile([P, 2, HALF, 4], BF16, align_bytes=64, name="ug", bufs=2)
            nc.scalar.copy(
                out=grouped[hb][:, :, r * P : (r + 1) * P, :].bitcast(F32),
                in_=ug[rt][:].rearrange("p (g u r) -> p g r u", g=2, u=2),
            )

        def quant_u(hb, g, r0, r1):
            c0 = hb * HALF
            nc.vector.quantize_mx(
                out=u_codes[:, g, c0 + r0 : c0 + r1].bitcast(FP8X4),
                scales=u_scales[:, g, c0 + r0 : c0 + r1],
                in_=grouped[hb][:, g, r0:r1, :].rearrange("p r t -> p (r t)"),
            )

        cbank = []

        def turn_c():
            cb = bank("o")
            for rt in range(8):
                nc.tensor.transpose(cb[:].bitcast(BF16)[:, rt * P : (rt + 1) * P], parts[:, rt, :], ident_b[:])
            cbank.append(cb)

        def copy_c():
            nc.scalar.copy(out=c_rows[:], in_=cbank[0][:].bitcast(BF16))

        pb = {}

        def bias_mm(rt, c, kind):
            pb[rt, c] = bank("o")
            cs = slice(c * HALF, (c + 1) * HALF)
            if kind == 1:
                nc.tensor.matmul(pb[rt, c][:], ident_b[:], x_t[:, rt, cs], start=True, stop=False)
            nc.tensor.matmul(
                pb[rt, c][:], c_rows[:, rt * P : (rt + 1) * P], brows[:, kind, cs], start=(kind == 0), stop=True
            )

        def scale_pre(rt, c):
            cs = slice(c * HALF, (c + 1) * HALF)
            nc.scalar.activation(out=pre[:, rt, cs], in_=pb[rt, c][:], func=ACT.Copy, scale=c_skip[:, rt : rt + 1])

        def make_pre(rt, c):
            cs = slice(c * HALF, (c + 1) * HALF)
            nc.vector.scalar_tensor_tensor(
                out=pre[:, rt, cs],
                in0=x_t[:, rt, cs],
                scalar=c_skip[:, rt : rt + 1],
                in1=pb[rt, c][:],
                op0=ALU.mult,
                op1=ALU.add,
            )

        def stage1(k, col0, tag):
            hb, j, r0, n = units[k]
            r0 += hb * HALF
            b = bank(tag)
            c0 = col0 + P * j
            for g in range(2):
                nc.tensor.matmul_mx(
                    out=b[:, 0:n],
                    lhsT=w1[:, g, 2 * c0 : 2 * (c0 + P)].bitcast(FP4X4),
                    lhsT_scale=w1s[:, g, c0 : c0 + P],
                    rhs=u_codes[:, g, r0 : r0 + n].bitcast(FP8X4),
                    rhs_scale=u_scales[:, g, r0 : r0 + n],
                    start=(g == 0),
                    stop=(g == 1),
                )
            return b

        units = [(0, j, 0, HALF) for j in range(NF)] + [(1, j, 0, HALF) for j in range(8)]
        if S["split"]:
            units += [(1, j, r0, 256) for r0 in (0, 256) for j in range(8, NF)]
        else:
            units += [(1, j, 0, HALF) for j in range(8, NF)]
        UNITS = len(units)
        gate, value, t_of, z_of, s_of = {}, {}, {}, {}, {}
        hd, hg, h_of = {}, {}, {}

        def op_gate(k):
            gate[k] = stage1(k, 0, "g")

        def op_value(k):
            value[k] = stage1(k, F, "v")

        def op_t(k):
            hb, j, r0, n = units[k]
            t = work.tile([P, HALF], F32, align_bytes=64, name="t", bufs=4)
            nc.scalar.activation(
                out=t[:, 0:n], in_=gate[k][:, 0:n], func=ACT.Identity, scale=cols[:, 0, j : j + 1], bias=cols[:, 1, j : j + 1]
            )
            t_of[k] = t

        def op_t2(k):
            hb, j, r0, n = units[k]
            r0 += hb * HALF
            t2 = work.tile([P, HALF], F32, align_bytes=64, name="t2", bufs=4)
            nc.gpsimd.tensor_tensor(out=t2[:, 0:n], in0=t_of[k][:, 0:n], in1=cn[:, r0 : r0 + n], op=ALU.mult)
            t_of[k] = t2

        def op_z(k):
            z = work.tile([P, HALF], F32, align_bytes=64, name="z", bufs=4)
            n = units[k][3]
            nc.vector.tensor_tensor(out=z[:, 0:n], in0=gate[k][:, 0:n], in1=t_of[k][:, 0:n], op=ALU.add)
            z_of[k] = z

        def op_s(k):
            hb, j, r0, n = units[k]
            s = work.tile([P, HALF], F32, align_bytes=64, name="s", bufs=4)
            nc.scalar.activation(out=s[:, 0:n], in_=z_of[k][:, 0:n], func=ACT.Silu, bias=cols[:, 2, j : j + 1])
            s_of[k] = s

        def op_h(k):
            hb, j, r0, n = units[k]
            h = work.tile([P, HALF], BF16, align_bytes=64, name="h", bufs=6)
            nc.vector.scalar_tensor_tensor(
                out=h[:, 0:n],
                in0=value[k][:, 0:n],
                scalar=cols[:, 3, j : j + 1],
                in1=s_of[k][:, 0:n],
                op0=ALU.add,
                op1=ALU.mult,
            )
            g, jj = divmod(j, 4)
            if (hb, g) not in hd:
                hd[hb, g] = work.tile([P, 4, HALF], BF16, align_bytes=64, name="hd")
            for t in range(4):
                nc.sync.dma_start(out=hd[hb, g][32 * jj : 32 * jj + 32, t, r0 : r0 + n], in_=h[t:P:4, 0:n])

        def weave(q, eng, r0, r1):
            if q not in hg:
                hg[q] = work.tile([P, HALF, 4], BF16, align_bytes=64, name="hg")
            dst = hg[q][:, r0:r1, :]
            src = hd[divmod(q, 3)][:, :, r0:r1].rearrange("p t r -> p r t")
            if eng == "g":
                nc.gpsimd.tensor_scalar(out=dst, in0=src, scalar1=1.0, scalar2=0.0, op0=ALU.mult, op1=ALU.add)
            elif eng == "a":
                nc.scalar.copy(out=dst, in_=src)
            else:
                nc.vector.tensor_copy(out=dst, in_=src)

        def quant_h(q, r0, r1):
            hb, g = divmod(q, 3)
            nc.vector.quantize_mx(
                out=h_codes[:, hb, g, r0:r1].bitcast(FP8X4),
                scales=h_scales[:, hb, g, r0:r1],
                in_=hg[q][:, r0:r1, :].rearrange("p r t -> p (r t)"),
            )

        obank = {}

        def stage2(hb, i, gs, tag=None):
            r, c = divmod(i, 2)
            if tag is not None:
                obank[hb, i] = bank(tag)
            for g in gs:
                nc.tensor.matmul_mx(
                    out=obank[hb, i][:],
                    lhsT=h_codes[:, hb, g, r * P : (r + 1) * P].bitcast(FP8X4),
                    lhsT_scale=h_scales[:, hb, g, r * P : (r + 1) * P],
                    rhs=w2[:, g, c * HALF : (c + 1) * HALF].bitcast(FP8X4),
                    rhs_scale=w2s[:, g, c * HALF : (c + 1) * HALF],
                    start=(g == 0),
                    stop=(g == 2),
                )

        def store(rt, c, o):
            nc.sync.dma_start(out=out[rt * P : (rt + 1) * P, c * HALF : (c + 1) * HALF], in_=o[:])

        def finish(hb, i):
            r, c = divmod(i, 2)
            rt = 4 * hb + r
            o = work.tile([P, HALF], F32, align_bytes=64, name="o", bufs=8)
            nc.vector.scalar_tensor_tensor(
                out=o[:],
                in0=obank[hb, i][:],
                scalar=c_out[:, rt : rt + 1],
                in1=pre[:, rt, c * HALF : (c + 1) * HALF],
                op0=ALU.mult,
                op1=ALU.add,
            )
            store(rt, c, o)

        def finish_ag(hb, i):
            r, c = divmod(i, 2)
            rt = 4 * hb + r
            o1 = work.tile([P, HALF], F32, align_bytes=64, name="o1")
            o = work.tile([P, HALF], F32, align_bytes=64, name="o", bufs=8)
            nc.scalar.activation(out=o1[:], in_=obank[hb, i][:], func=ACT.Copy, scale=c_out[:, rt : rt + 1])
            nc.gpsimd.tensor_tensor(out=o[:], in0=o1[:], in1=pre[:, rt, c * HALF : (c + 1) * HALF], op=ALU.add)
            store(rt, c, o)

        late_coefficients()
        for rt in S["ga"]:
            gain_x(rt)
        late_loads()
        for rt in range(4):
            for c in range(2):
                make_u(rt, c, gbank[c][:])
            turn_u(rt, "ox"[rt % 2])
            copy_u(rt)
        for r in range(2):
            for g in range(2):
                quant_u(0, g, 2 * P * r, 2 * P * (r + 1))
        feature_columns()
        nc.scalar.activation(out=dummy[:, 1:2], in_=dummy[:, 0:1], func=ACT.Silu)

        table = {}

        def at(k, fn, *args):
            table.setdefault(k, []).append((fn, args))

        for n, rt in enumerate(range(4, 8)):
            if rt in S["ga"]:
                at(S["u"][n], scale_u, rt)
            else:
                at(S["u"][n], make_u_late, rt)
            at(S["turn"][n], turn_u, rt, "x")
            at(S["tc"][n], copy_u, rt)
        at(S["qu"], quant_u, 1, 0, 0, HALF)
        at(S["qu"], quant_u, 1, 1, 0, HALF)
        at(0, turn_c)
        at(0, copy_c)
        for n in range(16):
            rt, c = divmod(n, 2)
            kind = S["kind"][n]
            at(S["pre"][n], bias_mm, rt, c, kind)
            at(S["pre"][n] + 1, scale_pre if kind else make_pre, rt, c)
        for q in range(5):
            w = HALF // len(S["weave"][q])
            for n, k in enumerate(S["weave"][q]):
                at(k, weave, q, S["weng"][q][n], w * n, w * n + w)
            at(S["qh"][q], quant_h, q, 0, HALF)
        if S["split"]:
            for r in range(2):
                at(S["w5"][r], weave, 5, S["weng"][5][r], 128 * r, 128 * (r + 1))
                at(S["q5"][r], quant_h, 5, 128 * r, 128 * (r + 1))
            for i in range(4):
                at(S["s5"][i], stage2, 1, i, (0, 1, 2), "oxo"[i % 3])
                at(S["s5"][i] + 1, finish_ag if i in S["fag"] else finish, 1, i)
        for i in range(S["early"]):
            at(S["s2"][i], stage2, 0, i, (0, 1, 2), "o")
            at(S["s2"][i] + 1, finish_ag if i in S["fag0"] else finish, 0, i)

        def unit(fn, k):
            if 0 <= k < UNITS:
                fn(k)

        pe = (turn_u, turn_c, bias_mm, stage2)
        for k in range(-2, UNITS + 5):
            unit(op_z, k - 1)
            unit(op_s, k - 2)
            for fn, args in table.get(k, []):
                if fn in pe:
                    fn(*args)
            unit(op_gate, k + 2)
            unit(op_h, k - 3)
            unit(op_t, k + 1)
            unit(op_t2, k)
            unit(op_value, k - 1)
            for fn, args in table.get(k, []):
                if fn not in pe:
                    fn(*args)

        for i in range(S["early"], 8):
            stage2(0, i, (0, 1, 2), "oox"[i % 3])
            (finish_ag if i in S["fag0"] else finish)(0, i)
        first = 4 if S["split"] else 0
        for i in range(first, 8):
            stage2(1, i, (0, 1), S["tags"][i])
        for r in range(first // 2, 4):
            weave(5, S["weng"][5][r], 128 * r, 128 * (r + 1))
        for r in range(first // 2, 4):
            quant_h(5, 128 * r, 128 * (r + 1))
        for i in range(first, 8):
            stage2(1, i, (2,))
            (finish_ag if i in S["fag"] else finish)(1, i)
